import numpy as np, ml_dtypes
CORES = [33,38,57,62,81,86,161,166,185,190,209,214]
N = 12
DEG, TK, TIMES = 3, 256, 2
MASK = [[0,9,11],[1,3,11],[2,3,5],[0,3,7],[4,7,9],[5,7,11],[2,6,8],[2,6,7],[8,9,10],[3,9,11],[0,1,10],[3,4,11]]
def setup_inputs(rng):
    return {"x": rng.standard_normal((N, 128, TK), dtype=np.float32).astype(ml_dtypes.bfloat16), "w": (rng.standard_normal((N, 128, DEG * 128), dtype=np.float32) / np.float32(np.sqrt(128 * DEG / 2))).astype(ml_dtypes.bfloat16)}
def setup_inputs_big(rng):
    d = setup_inputs(rng)
    for k in ("x", "w"): d[k] = (d[k].astype(np.float32) * 1024.0).astype(d[k].dtype)
    return d
def setup_inputs_small(rng):
    d = setup_inputs(rng)
    for k in ("x", "w"): d[k] = (d[k].astype(np.float32) * (1 / 1024.0)).astype(d[k].dtype)
    return d
def setup_inputs_apart(rng):
    d = setup_inputs(rng)
    f = (10.0 ** rng.permutation(np.linspace(-1.5, 1.5, N))).astype(np.float32).reshape(N, 1, 1)
    for k in ("x", "w"): d[k] = (d[k].astype(np.float32) * f).astype(d[k].dtype)
    return d
def reference(x, w):
    X, W = x.astype(np.float64), w.astype(np.float64)
    h = list(X)
    for _ in range(TIMES):
        h = [np.maximum(sum(W[r][:, 128 * i:128 * i + 128].T @ h[j] for i, j in enumerate(MASK[r])), 0.0) for r in range(N)]
    return {"y": np.stack(h).astype(ml_dtypes.bfloat16)}

@@ -1,0 +1,247 @@
+from concourse.bass import DstId, RemoteDMATransfer
+from concourse.mybir import AluOpType
+
+CFG = {"mode": "balance", "deleg": True, "kpre": None, "hmax": 99, "e_off": 8, "e_on": 8, "on_sep": True, "multi": True}
+
+NRANK, ND, NP, TK = 12, 12, 3, 256
+SCRATCH = {"zero": ("sbuf", [128, TK], "float32"),
+           "w0": ("sbuf", [128, 384], "bfloat16"), "w1": ("sbuf", [128, 384], "bfloat16")}
+for _i in range(ND):
+    SCRATCH["d%d" % _i] = ("sbuf", [128, TK], "bfloat16")
+for _i in range(NP):
+    SCRATCH["p%d" % _i] = ("psum", [128, 512], "float32")
+SEMAPHORES = ["zs", "sent", "st"] + ["mm%d" % _i for _i in range(NP)]
+for _k in "xwhy":
+    SEMAPHORES += ["s%s%d" % (_k, _i) for _i in range(NRANK)]
+
+ON, OFF, CMP = 1.0, 1.5, 0.5
+
+
+def build(T, topo, cfg):
+    cores = list(T.cores)
+    M = T.tables["MASK"]
+    N = len(cores)
+
+    def onchip(a, b):
+        return topo.host(a) == topo.host(b) and topo.chip(a) == topo.chip(b)
+
+    def hop(a, b):
+        return ON if onchip(a, b) else OFF
+
+    edges = sorted((j, r) for r in range(N) for j in M[r] if j != r)
+    load = {}
+    for j, r in edges:
+        if topo.may_write(cores[j], cores[r]) and not onchip(cores[j], cores[r]):
+            load[cores[j]] = load.get(cores[j], 0) + 1
+    relay = {}
+    for j, r in edges:
+        a, b = cores[j], cores[r]
+        if topo.may_write(a, b):
+            continue
+        mode = cfg["mode"]
+        if mode != "helper" and min(load.get(c, 0) for c in cores if c != a and c != b and topo.may_write(a, c)
+                                    and topo.may_write(c, b)) >= cfg["hmax"]:
+            mode = "helper"
+        if mode == "helper":
+            pool = [c for c in range(max(a - 8, 0), a + 9) if onchip(a, c) and c not in cores]
+        else:
+            pool = cores
+        pool = [c for c in pool if c != a and c != b and topo.may_write(a, c) and topo.may_write(c, b)]
+        if mode == "partner":
+            key = lambda c: (not onchip(a, c), load.get(c, 0), c)
+        elif mode == "helper":
+            key = lambda c: (load.get(c, 0), topo.die(c) != topo.die(a), c)
+        else:
+            key = lambda c: (load.get(c, 0), not onchip(a, c), c)
+        c = min(pool, key=key)
+        relay[(j, r)] = c
+        load[c] = load.get(c, 0) + 1
+    site = dict((j, cores[j]) for j in range(N))
+    if cfg["deleg"]:
+        for j in range(N):
+            rin = [k for k in M[j] if (k, j) in relay]
+            rout = [relay[e] for e in sorted(relay) if e[0] == j and onchip(relay[e], cores[j])]
+            if rin and rout:
+                site[j] = rout[0]
+    src_of = {}
+
+    def path(item, a, b, via):
+        if a == b:
+            return
+        if via is None or via == b:
+            src_of.setdefault((item, b), a)
+        else:
+            src_of.setdefault((item, via), a)
+            src_of.setdefault((item, b), via)
+
+    tasks = {}
+    for j in range(N):
+        s = site[j]
+        for k in M[j]:
+            path("x%d" % k, cores[k], s, None if topo.may_write(cores[k], s) else relay[(k, j)])
+        path("w%d" % j, cores[j], s, None)
+        tasks.setdefault(s, []).append(("h%d" % j, "w%d" % j, [(i, "x%d" % k) for i, k in enumerate(M[j])]))
+    for r in range(N):
+        for j in M[r]:
+            path("h%d" % j, site[j], cores[r], None if topo.may_write(site[j], cores[r]) else relay[(j, r)])
+        tasks.setdefault(cores[r], []).append(("y%d" % r, "w%d" % r, [(i, "h%d" % j) for i, j in enumerate(M[r])]))
+    prod = {}
+    for c in tasks:
+        for out, w, ops in tasks[c]:
+            prod[(out, c)] = [it for _, it in ops] + [w]
+    memo = {}
+
+    def avail(item, c):
+        k = (item, c)
+        if k not in memo:
+            if k in src_of:
+                memo[k] = avail(item, src_of[k]) + hop(src_of[k], c)
+            elif k in prod:
+                memo[k] = max(avail(it, c) for it in prod[k]) + CMP
+            else:
+                memo[k] = 0.0
+        return memo[k]
+
+    fin = max(avail("y%d" % r, cores[r]) for r in range(N))
+    memo2 = {}
+
+    def need(item, c):
+        k = (item, c)
+        if k not in memo2:
+            v = fin
+            for (it, b), a in src_of.items():
+                if it == item and a == c:
+                    v = min(v, need(it, b) - hop(c, b))
+            for out, w, ops in tasks.get(c, []):
+                if item in prod[(out, c)]:
+                    v = min(v, need(out, c) - CMP)
+            memo2[k] = v
+        return memo2[k]
+
+    plan = {}
+    used = set(cores) | set(a for a in src_of.values()) | set(b for _, b in src_of)
+    for c in sorted(used):
+        sends = {}
+        for (it, b), a in sorted(src_of.items()):
+            if a == c:
+                sends.setdefault(it, []).append((need(it, b) - hop(c, b) - avail(it, c), b))
+        own = None if c not in cores else "x%d" % cores.index(c)
+        fwd = [it for it in sends if it[0] == "x" and it != own]
+        calls = []
+        for it in sends:
+            ds = sorted(sends[it])
+            if it == own and fwd and cfg["kpre"] is not None:
+                first = [d for d in ds if d[0] < 0.01 or (cfg["on_sep"] and onchip(c, d[1]))]
+                rest = [d for d in ds if d not in first]
+                first, rest = first + rest[:cfg["kpre"]], rest[cfg["kpre"]:]
+                if first:
+                    calls.append(((0, 0.0, 0.0), it, [b for _, b in first]))
+                if rest:
+                    calls.append(((2, 0.0, 0.0), it, [b for _, b in rest]))
+            else:
+                ph = {"x": 0 if it == own else 1, "w": 3, "h": 4}[it[0]]
+                calls.append(((ph, avail(it, c), ds[0][0]), it, [b for _, b in ds]))
+        calls.sort()
+        items = sorted(set([it for it, b in src_of if b == c] + [o for o, _, _ in tasks.get(c, [])]
+                           + ([own] if own else [])))
+        slot, nd = {}, 0
+        for it in items:
+            if it[0] == "w":
+                slot[it] = "w1"
+            else:
+                slot[it] = "d%d" % nd
+                nd += 1
+        if own:
+            slot["w" + own[1:]] = "w0"
+        ts = sorted(tasks.get(c, []), key=lambda t: avail(t[0], c))
+        ts = [(o, w, sorted(ops, key=lambda p: (avail(p[1], c), p[0]))) for o, w, ops in ts]
+        plan[c] = {"calls": [(it, ds) for _, it, ds in calls], "slot": slot, "tasks": ts}
+    cnt = {}
+    for (it, b), a in src_of.items():
+        sep = cfg["on_sep"] or not any((not onchip(a, bb)) for (i2, bb), aa in src_of.items() if aa == a)
+        cnt[(it, b)] = cfg["e_on"] if (onchip(a, b) and sep) else cfg["e_off"]
+    for k in prod:
+        cnt[k] = 1
+    for r in range(N):
+        cnt[("x%d" % r, cores[r])] = 16
+        cnt[("w%d" % r, cores[r])] = 16
+    return plan, cnt, onchip
+
+
+def pick(mask, n):
+    out, b = 0, 1
+    while n and b <= mask:
+        if mask & b:
+            out |= b
+            n -= 1
+        b <<= 1
+    return out
+
+
+def rank_program(g, core, T, topo):
+    cfg = CFG
+    plan, cnt, onchip = build(T, topo, cfg)
+    if core not in plan:
+        return
+    me = plan[core]
+    rank = T.rank_of(core)
+
+    def buf(it, c=core):
+        return T[plan[c]["slot"][it]]
+
+    def sem(it):
+        return T.sem["s" + it]
+
+    if rank is not None:
+        g.sync.dma_start(buf("x%d" % rank)[:], T.x[:]).then_inc(sem("x%d" % rank), 16)
+        g.sync.dma_start(buf("w%d" % rank)[:], T.w[:]).then_inc(sem("w%d" % rank), 16)
+    if me["tasks"]:
+        g.vector.memset(T.zero[:], 0.0).then_inc(T.sem.zs, 1)
+        g.vector.wait_ge(T.sem.zs, 1)
+
+    offs = [b for _, ds in me["calls"] for b in ds if not onchip(core, b)]
+    offmask = 0
+    for b in offs:
+        offmask |= topo.mask(core, b)
+    total = 0
+    for it, ds in me["calls"]:
+        g.wait_ge(sem(it), cnt[(it, core)])
+        groups = {}
+        for b in ds:
+            n = cnt[(it, b)]
+            if onchip(core, b) and (cfg["on_sep"] or not offs):
+                m = pick(topo.mask(core, b) & ~offmask, n)
+            else:
+                m = pick(topo.mask(core, b), n)
+            groups.setdefault(m, []).append(b)
+        if cfg["multi"]:
+            trs = []
+            for m in sorted(groups):
+                ids = [topo.addr(b, core) for b in groups[m]]
+                trs.append(RemoteDMATransfer(dst_ids=[DstId(rid=a[0], pnc=a[1]) for a in ids], dma_engine_mask=m,
+                                             remote_sem=sem(it), srcs=[buf(it)[:]],
+                                             dsts=[buf(it, b)[:] for b in groups[m]]))
+                total += cnt[(it, groups[m][0])]
+            g.remote_dma_fused(trs, local_sem=T.sem.sent)
+        else:
+            for b in ds:
+                m = [mm for mm in groups if b in groups[mm]][0]
+                rid, pid = topo.addr(b, core)
+                g.remote_dma(buf(it, b)[:], buf(it)[:], sem(it), T.sem.sent, pid, rid, m)
+                total += cnt[(it, b)]
+    if total:
+        g.wait_ge(T.sem.sent, total)
+
+    for ti, (out, w, ops) in enumerate(me["tasks"]):
+        ps = T["p%d" % ti][:, 0:TK]
+        g.tensor.wait_ge(sem(w), cnt[(w, core)])
+        for n, (i, it) in enumerate(ops):
+            g.tensor.wait_ge(sem(it), cnt[(it, core)])
+            g.tensor.matmul(ps, buf(w)[:, 128 * i:128 * i + 128], buf(it)[:], start=(n == 0),
+                            stop=(n == len(ops) - 1)).then_inc(T.sem["mm%d" % ti], 1)
+        g.vector.wait_ge(T.sem["mm%d" % ti], len(ops))
+        g.vector.tensor_tensor(buf(out)[:], ps, T.zero[:], AluOpType.max).then_inc(sem(out), 1)
+    if rank is not None:
+        g.sync.wait_ge(sem("y%d" % rank), 1)
+        g.sync.dma_start(T.y[:], buf("y%d" % rank)[:]).then_inc(T.sem.st, 16)
+        g.sync.wait_ge(T.sem.st, 16)

@@ -1,247 +1,151 @@
 from concourse.bass import DstId, RemoteDMATransfer
 from concourse.mybir import AluOpType
 
-CFG = {"mode": "balance", "deleg": True, "kpre": None, "hmax": 99, "e_off": 8, "e_on": 8, "on_sep": True, "multi": True}
+NRANK, TK, WK, NBANK = 12, 256, 384, 4
+CALLS = {
+    0: [("x0", [(1, "A"), (11, "A")]), ("w0", [(1, "B")])],
+    1: [("x1", [(11, "A")]), ("x0", [(3, "A")]), ("h0", [(10, "A")]), ("h0", [(3, "A")]), ("h0", [(0, "B")]),
+        ("h1", [(10, "A")]), ("h11", [(0, "F")])],
+    2: [("x2", [(9, "A")]), ("x2", [(3, "F")]), ("w2", [(3, "F")])],
+    3: [("x3", [(9, "A")]), ("x3", [(11, "A")]), ("x3", [(1, "A")]), ("x3", [(2, "B")]), ("x2", [(7, "A")]),
+        ("h2", [(6, "A")]), ("h3", [(1, "A"), (11, "A"), (9, "A"), (2, "B")])],
+    4: [("x4", [(11, "A")]), ("xw4", [(5, "B")]), ("x4", [(1, "A")])],
+    5: [("x5", [(2, "A")]), ("x5", [(3, "A")]), ("h4", [(11, "A")]), ("h4", [(4, "B")]), ("h5", [(2, "A")])],
+    6: [("x6", [(7, "F")]), ("h7", [(4, "A")]), ("h6", [(7, "B")]), ("h2", [(7, "F")])],
+    7: [("x7", [(3, "A")]), ("x7", [(5, "A")]), ("xw7", [(6, "B")]), ("h7", [(5, "A")]), ("h7", [(3, "A")])],
+    8: [("x8", [(9, "F")]), ("w8", [(9, "B")])],
+    9: [("x9", [(1, "A"), (5, "A")]), ("x2", [(6, "A")]), ("x8", [(6, "A")]), ("h9", [(4, "A")]), ("h9", [(0, "A")]),
+        ("h8", [(6, "A")]), ("h9", [(8, "B")]), ("h8", [(8, "F")])],
+    10: [("x10", [(11, "A")]), ("w10", [(11, "A")])],
+    11: [("x11", [(9, "A")]), ("x11", [(1, "A")]), ("x10", [(9, "A")]), ("x11", [(5, "A")]), ("w11", [(1, "A")]),
+         ("h10", [(10, "B")]), ("h11", [(5, "A"), (9, "A")]), ("h10", [(8, "A")])],
+}
+MM = {
+    0: [("y0", 0), ("y0", 1), ("y0", 2)],
+    1: [("h1", 0), ("h0", 0), ("h0", 1), ("h0", 2), ("h1", 2), ("h1", 1), ("y1", 0), ("h11", 0), ("h11", 1),
+        ("h11", 2), ("y1", 2), ("y1", 1)],
+    2: [("h2", 0), ("h2", 2), ("h2", 1), ("y2", 0), ("y2", 1), ("y2", 2)],
+    3: [("h3", 1), ("h3", 2), ("h2", 0), ("h2", 1), ("h2", 2), ("h3", 0), ("y3", 1), ("y3", 0), ("y3", 2)],
+    4: [("y4", 2), ("y4", 0), ("y4", 1)],
+    5: [("h5", 0), ("h4", 0), ("h4", 1), ("h4", 2), ("h5", 1), ("h5", 2), ("y5", 0), ("y5", 2), ("y5", 1)],
+    6: [("h6", 1), ("h7", 1), ("h7", 2), ("h6", 0), ("h7", 0), ("h6", 2), ("y6", 0), ("y6", 1), ("y6", 2)],
+    7: [("h7", 2), ("h7", 1), ("h7", 0), ("y7", 2), ("y7", 1), ("y7", 0)],
+    8: [("y8", 1), ("y8", 0), ("y8", 2)],
+    9: [("h9", 1), ("h9", 0), ("h9", 2), ("h8", 0), ("h8", 1), ("y9", 1), ("h8", 2), ("y9", 2), ("y9", 0)],
+    10: [("y10", 2), ("y10", 0), ("y10", 1)],
+    11: [("h11", 2), ("h11", 1), ("h10", 1), ("h10", 2), ("h10", 0), ("h11", 0), ("y11", 2), ("y11", 1), ("y11", 0)],
+}
 
-NRANK, ND, NP, TK = 12, 12, 3, 256
-SCRATCH = {"zero": ("sbuf", [128, TK], "float32"),
-           "w0": ("sbuf", [128, 384], "bfloat16"), "w1": ("sbuf", [128, 384], "bfloat16")}
-for _i in range(ND):
-    SCRATCH["d%d" % _i] = ("sbuf", [128, TK], "bfloat16")
-for _i in range(NP):
+SCRATCH = {"zero": ("sbuf", [128, TK], "float32"), "yy": ("sbuf", [128, TK], "bfloat16")}
+for _i in range(NRANK):
+    SCRATCH["xw%d" % _i] = ("sbuf", [128, TK + WK], "bfloat16")
+    SCRATCH["h%d" % _i] = ("sbuf", [128, TK], "bfloat16")
+for _i in range(NBANK):
     SCRATCH["p%d" % _i] = ("psum", [128, 512], "float32")
-SEMAPHORES = ["zs", "sent", "st"] + ["mm%d" % _i for _i in range(NP)]
-for _k in "xwhy":
+SEMAPHORES = ["zs", "sent", "st", "sy"] + ["mm%d" % _i for _i in range(NBANK)]
+for _k in "xwh":
     SEMAPHORES += ["s%s%d" % (_k, _i) for _i in range(NRANK)]
 
-ON, OFF, CMP = 1.0, 1.5, 0.5
+
+def parts(it):
+    return ["x" + it[2:], "w" + it[2:]] if it[:2] == "xw" else [it]
 
 
-def build(T, topo, cfg):
-    cores = list(T.cores)
-    M = T.tables["MASK"]
-    N = len(cores)
-
-    def onchip(a, b):
-        return topo.host(a) == topo.host(b) and topo.chip(a) == topo.chip(b)
-
-    def hop(a, b):
-        return ON if onchip(a, b) else OFF
-
-    edges = sorted((j, r) for r in range(N) for j in M[r] if j != r)
-    load = {}
-    for j, r in edges:
-        if topo.may_write(cores[j], cores[r]) and not onchip(cores[j], cores[r]):
-            load[cores[j]] = load.get(cores[j], 0) + 1
-    relay = {}
-    for j, r in edges:
-        a, b = cores[j], cores[r]
-        if topo.may_write(a, b):
-            continue
-        mode = cfg["mode"]
-        if mode != "helper" and min(load.get(c, 0) for c in cores if c != a and c != b and topo.may_write(a, c)
-                                    and topo.may_write(c, b)) >= cfg["hmax"]:
-            mode = "helper"
-        if mode == "helper":
-            pool = [c for c in range(max(a - 8, 0), a + 9) if onchip(a, c) and c not in cores]
-        else:
-            pool = cores
-        pool = [c for c in pool if c != a and c != b and topo.may_write(a, c) and topo.may_write(c, b)]
-        if mode == "partner":
-            key = lambda c: (not onchip(a, c), load.get(c, 0), c)
-        elif mode == "helper":
-            key = lambda c: (load.get(c, 0), topo.die(c) != topo.die(a), c)
-        else:
-            key = lambda c: (load.get(c, 0), not onchip(a, c), c)
-        c = min(pool, key=key)
-        relay[(j, r)] = c
-        load[c] = load.get(c, 0) + 1
-    site = dict((j, cores[j]) for j in range(N))
-    if cfg["deleg"]:
-        for j in range(N):
-            rin = [k for k in M[j] if (k, j) in relay]
-            rout = [relay[e] for e in sorted(relay) if e[0] == j and onchip(relay[e], cores[j])]
-            if rin and rout:
-                site[j] = rout[0]
-    src_of = {}
-
-    def path(item, a, b, via):
-        if a == b:
-            return
-        if via is None or via == b:
-            src_of.setdefault((item, b), a)
-        else:
-            src_of.setdefault((item, via), a)
-            src_of.setdefault((item, b), via)
-
-    tasks = {}
-    for j in range(N):
-        s = site[j]
-        for k in M[j]:
-            path("x%d" % k, cores[k], s, None if topo.may_write(cores[k], s) else relay[(k, j)])
-        path("w%d" % j, cores[j], s, None)
-        tasks.setdefault(s, []).append(("h%d" % j, "w%d" % j, [(i, "x%d" % k) for i, k in enumerate(M[j])]))
-    for r in range(N):
-        for j in M[r]:
-            path("h%d" % j, site[j], cores[r], None if topo.may_write(site[j], cores[r]) else relay[(j, r)])
-        tasks.setdefault(cores[r], []).append(("y%d" % r, "w%d" % r, [(i, "h%d" % j) for i, j in enumerate(M[r])]))
-    prod = {}
-    for c in tasks:
-        for out, w, ops in tasks[c]:
-            prod[(out, c)] = [it for _, it in ops] + [w]
-    memo = {}
-
-    def avail(item, c):
-        k = (item, c)
-        if k not in memo:
-            if k in src_of:
-                memo[k] = avail(item, src_of[k]) + hop(src_of[k], c)
-            elif k in prod:
-                memo[k] = max(avail(it, c) for it in prod[k]) + CMP
-            else:
-                memo[k] = 0.0
-        return memo[k]
-
-    fin = max(avail("y%d" % r, cores[r]) for r in range(N))
-    memo2 = {}
-
-    def need(item, c):
-        k = (item, c)
-        if k not in memo2:
-            v = fin
-            for (it, b), a in src_of.items():
-                if it == item and a == c:
-                    v = min(v, need(it, b) - hop(c, b))
-            for out, w, ops in tasks.get(c, []):
-                if item in prod[(out, c)]:
-                    v = min(v, need(out, c) - CMP)
-            memo2[k] = v
-        return memo2[k]
-
-    plan = {}
-    used = set(cores) | set(a for a in src_of.values()) | set(b for _, b in src_of)
-    for c in sorted(used):
-        sends = {}
-        for (it, b), a in sorted(src_of.items()):
-            if a == c:
-                sends.setdefault(it, []).append((need(it, b) - hop(c, b) - avail(it, c), b))
-        own = None if c not in cores else "x%d" % cores.index(c)
-        fwd = [it for it in sends if it[0] == "x" and it != own]
-        calls = []
-        for it in sends:
-            ds = sorted(sends[it])
-            if it == own and fwd and cfg["kpre"] is not None:
-                first = [d for d in ds if d[0] < 0.01 or (cfg["on_sep"] and onchip(c, d[1]))]
-                rest = [d for d in ds if d not in first]
-                first, rest = first + rest[:cfg["kpre"]], rest[cfg["kpre"]:]
-                if first:
-                    calls.append(((0, 0.0, 0.0), it, [b for _, b in first]))
-                if rest:
-                    calls.append(((2, 0.0, 0.0), it, [b for _, b in rest]))
-            else:
-                ph = {"x": 0 if it == own else 1, "w": 3, "h": 4}[it[0]]
-                calls.append(((ph, avail(it, c), ds[0][0]), it, [b for _, b in ds]))
-        calls.sort()
-        items = sorted(set([it for it, b in src_of if b == c] + [o for o, _, _ in tasks.get(c, [])]
-                           + ([own] if own else [])))
-        slot, nd = {}, 0
-        for it in items:
-            if it[0] == "w":
-                slot[it] = "w1"
-            else:
-                slot[it] = "d%d" % nd
-                nd += 1
-        if own:
-            slot["w" + own[1:]] = "w0"
-        ts = sorted(tasks.get(c, []), key=lambda t: avail(t[0], c))
-        ts = [(o, w, sorted(ops, key=lambda p: (avail(p[1], c), p[0]))) for o, w, ops in ts]
-        plan[c] = {"calls": [(it, ds) for _, it, ds in calls], "slot": slot, "tasks": ts}
-    cnt = {}
-    for (it, b), a in src_of.items():
-        sep = cfg["on_sep"] or not any((not onchip(a, bb)) for (i2, bb), aa in src_of.items() if aa == a)
-        cnt[(it, b)] = cfg["e_on"] if (onchip(a, b) and sep) else cfg["e_off"]
-    for k in prod:
-        cnt[k] = 1
-    for r in range(N):
-        cnt[("x%d" % r, cores[r])] = 16
-        cnt[("w%d" % r, cores[r])] = 16
-    return plan, cnt, onchip
-
-
-def pick(mask, n):
-    out, b = 0, 1
-    while n and b <= mask:
-        if mask & b:
-            out |= b
-            n -= 1
-        b <<= 1
-    return out
+def bits(m):
+    n = 0
+    while m:
+        n += m & 1
+        m >>= 1
+    return n
 
 
 def rank_program(g, core, T, topo):
-    cfg = CFG
-    plan, cnt, onchip = build(T, topo, cfg)
-    if core not in plan:
-        return
-    me = plan[core]
     rank = T.rank_of(core)
+    if rank is None:
+        return
+    cores = list(T.cores)
+    M = T.tables["MASK"]
 
-    def buf(it, c=core):
-        return T[plan[c]["slot"][it]]
+    def sets(c):
+        every, wide = ~0, 0
+        for b in cores:
+            if b != c and topo.may_write(c, b):
+                every &= topo.mask(c, b)
+                wide |= topo.mask(c, b)
+        return {"A": every, "B": wide & ~every, "F": wide}
 
-    def sem(it):
-        return T.sem["s" + it]
+    def ap(it):
+        j = it[2:] if it[:2] == "xw" else it[1:]
+        if it[:2] == "xw":
+            return T["xw" + j][:]
+        if it[0] == "x":
+            return T["xw" + j][:, 0:TK]
+        if it[0] == "w":
+            return T["xw" + j][:, TK:TK + WK]
+        return T["h" + j][:]
 
-    if rank is not None:
-        g.sync.dma_start(buf("x%d" % rank)[:], T.x[:]).then_inc(sem("x%d" % rank), 16)
-        g.sync.dma_start(buf("w%d" % rank)[:], T.w[:]).then_inc(sem("w%d" % rank), 16)
-    if me["tasks"]:
-        g.vector.memset(T.zero[:], 0.0).then_inc(T.sem.zs, 1)
-        g.vector.wait_ge(T.sem.zs, 1)
+    have = {"x%d" % rank: ("sx%d" % rank, 16), "w%d" % rank: ("sw%d" % rank, 16)}
+    for s in CALLS:
+        for it, ds in CALLS[s]:
+            for d, gp in ds:
+                if d == rank:
+                    for p in parts(it):
+                        have[p] = ("s" + parts(it)[0], bits(sets(cores[s])[gp]))
+    outs = []
+    for o, _ in MM[rank]:
+        if o not in outs:
+            outs.append(o)
+            have[o] = ("sy", 1) if o[0] == "y" else ("s" + o, 1)
 
-    offs = [b for _, ds in me["calls"] for b in ds if not onchip(core, b)]
-    offmask = 0
-    for b in offs:
-        offmask |= topo.mask(core, b)
+    def wait(q, it):
+        for p in parts(it):
+            q.wait_ge(T.sem[have[p][0]], have[p][1])
+
+    g.sync.dma_start(ap("x%d" % rank), T.x[:]).then_inc(T.sem["sx%d" % rank], 16)
+    g.sync.dma_start(ap("w%d" % rank), T.w[:]).then_inc(T.sem["sw%d" % rank], 16)
+    g.vector.memset(T.zero[:], 0.0).then_inc(T.sem.zs, 1)
+    g.vector.wait_ge(T.sem.zs, 1)
+
+    mine = sets(core)
     total = 0
-    for it, ds in me["calls"]:
-        g.wait_ge(sem(it), cnt[(it, core)])
+    for it, ds in CALLS[rank]:
+        wait(g, it)
         groups = {}
-        for b in ds:
-            n = cnt[(it, b)]
-            if onchip(core, b) and (cfg["on_sep"] or not offs):
-                m = pick(topo.mask(core, b) & ~offmask, n)
-            else:
-                m = pick(topo.mask(core, b), n)
-            groups.setdefault(m, []).append(b)
-        if cfg["multi"]:
-            trs = []
-            for m in sorted(groups):
-                ids = [topo.addr(b, core) for b in groups[m]]
-                trs.append(RemoteDMATransfer(dst_ids=[DstId(rid=a[0], pnc=a[1]) for a in ids], dma_engine_mask=m,
-                                             remote_sem=sem(it), srcs=[buf(it)[:]],
-                                             dsts=[buf(it, b)[:] for b in groups[m]]))
-                total += cnt[(it, groups[m][0])]
-            g.remote_dma_fused(trs, local_sem=T.sem.sent)
-        else:
-            for b in ds:
-                m = [mm for mm in groups if b in groups[mm]][0]
-                rid, pid = topo.addr(b, core)
-                g.remote_dma(buf(it, b)[:], buf(it)[:], sem(it), T.sem.sent, pid, rid, m)
-                total += cnt[(it, b)]
-    if total:
-        g.wait_ge(T.sem.sent, total)
+        for d, gp in ds:
+            b = cores[d]
+            if not topo.may_write(core, b) or mine[gp] & ~topo.mask(core, b):
+                raise ValueError("rank %d may not write to rank %d on engine set %s" % (rank, d, gp))
+            groups.setdefault(mine[gp], []).append(b)
+        trs = []
+        for m in sorted(groups):
+            ids = [topo.addr(b, core) for b in groups[m]]
+            trs.append(RemoteDMATransfer(dst_ids=[DstId(rid=a[0], pnc=a[1]) for a in ids], dma_engine_mask=m,
+                                         remote_sem=T.sem["s" + parts(it)[0]], srcs=[ap(it)],
+                                         dsts=[ap(it) for _ in groups[m]]))
+            total += bits(m)
+        g.remote_dma_fused(trs, local_sem=T.sem.sent)
+    g.wait_ge(T.sem.sent, total)
 
-    for ti, (out, w, ops) in enumerate(me["tasks"]):
-        ps = T["p%d" % ti][:, 0:TK]
-        g.tensor.wait_ge(sem(w), cnt[(w, core)])
-        for n, (i, it) in enumerate(ops):
-            g.tensor.wait_ge(sem(it), cnt[(it, core)])
-            g.tensor.matmul(ps, buf(w)[:, 128 * i:128 * i + 128], buf(it)[:], start=(n == 0),
-                            stop=(n == len(ops) - 1)).then_inc(T.sem["mm%d" % ti], 1)
-        g.vector.wait_ge(T.sem["mm%d" % ti], len(ops))
-        g.vector.tensor_tensor(buf(out)[:], ps, T.zero[:], AluOpType.max).then_inc(sem(out), 1)
-    if rank is not None:
-        g.sync.wait_ge(sem("y%d" % rank), 1)
-        g.sync.dma_start(T.y[:], buf("y%d" % rank)[:]).then_inc(T.sem.st, 16)
-        g.sync.wait_ge(T.sem.st, 16)
+    seen = {}
+    order = []
+    for o, i in MM[rank]:
+        j = int(o[1:])
+        op = ("x" if o[0] == "h" else "h") + "%d" % M[j][i]
+        ti = outs.index(o)
+        n = seen.get(o, 0)
+        seen[o] = n + 1
+        if n == 0:
+            wait(g.tensor, "w%d" % j)
+        wait(g.tensor, op)
+        g.tensor.matmul(T["p%d" % ti][:, 0:TK], T["xw%d" % j][:, TK + 128 * i:TK + 128 * i + 128], ap(op),
+                        start=(n == 0), stop=(n == 2)).then_inc(T.sem["mm%d" % ti], 1)
+        if n == 2:
+            order.append(o)
+    for o in order:
+        ti = outs.index(o)
+        g.vector.wait_ge(T.sem["mm%d" % ti], 3)
+        dst = T.yy[:] if o[0] == "y" else ap(o)
+        g.vector.tensor_tensor(dst, T["p%d" % ti][:, 0:TK], T.zero[:], AluOpType.max).then_inc(T.sem[have[o][0]], 1)
+    g.sync.wait_ge(T.sem.sy, 1)
+    g.sync.dma_start(T.y[:], T.yy[:]).then_inc(T.sem.st, 16)
+    g.sync.wait_ge(T.sem.st, 16)

from concourse.bass import DstId, RemoteDMATransfer
from concourse.mybir import AluOpType

NRANK, TK, WK, NBANK = 12, 256, 384, 4
CALLS = {
    0: [("x0", [(1, "A"), (11, "A")]), ("w0", [(1, "B")])],
    1: [("x1", [(11, "A")]), ("x0", [(3, "A")]), ("h0", [(10, "A")]), ("h0", [(3, "A")]), ("h0", [(0, "B")]),
        ("h1", [(10, "A")]), ("h11", [(0, "F")])],
    2: [("x2", [(9, "A")]), ("x2", [(3, "F")]), ("w2", [(3, "F")])],
    3: [("x3", [(9, "A")]), ("x3", [(11, "A")]), ("x3", [(1, "A")]), ("x3", [(2, "B")]), ("x2", [(7, "A")]),
        ("h2", [(6, "A")]), ("h3", [(1, "A"), (11, "A"), (9, "A"), (2, "B")])],
    4: [("x4", [(11, "A")]), ("xw4", [(5, "B")]), ("x4", [(1, "A")])],
    5: [("x5", [(2, "A")]), ("x5", [(3, "A")]), ("h4", [(11, "A")]), ("h4", [(4, "B")]), ("h5", [(2, "A")])],
    6: [("x6", [(7, "F")]), ("h7", [(4, "A")]), ("h6", [(7, "B")]), ("h2", [(7, "F")])],
    7: [("x7", [(3, "A")]), ("x7", [(5, "A")]), ("xw7", [(6, "B")]), ("h7", [(5, "A")]), ("h7", [(3, "A")])],
    8: [("x8", [(9, "F")]), ("w8", [(9, "B")])],
    9: [("x9", [(1, "A"), (5, "A")]), ("x2", [(6, "A")]), ("x8", [(6, "A")]), ("h9", [(4, "A")]), ("h9", [(0, "A")]),
        ("h8", [(6, "A")]), ("h9", [(8, "B")]), ("h8", [(8, "F")])],
    10: [("x10", [(11, "A")]), ("w10", [(11, "A")])],
    11: [("x11", [(9, "A")]), ("x11", [(1, "A")]), ("x10", [(9, "A")]), ("x11", [(5, "A")]), ("w11", [(1, "A")]),
         ("h10", [(10, "B")]), ("h11", [(5, "A"), (9, "A")]), ("h10", [(8, "A")])],
}
MM = {
    0: [("y0", 0), ("y0", 1), ("y0", 2)],
    1: [("h1", 0), ("h0", 0), ("h0", 1), ("h0", 2), ("h1", 2), ("h1", 1), ("y1", 0), ("h11", 0), ("h11", 1),
        ("h11", 2), ("y1", 2), ("y1", 1)],
    2: [("h2", 0), ("h2", 2), ("h2", 1), ("y2", 0), ("y2", 1), ("y2", 2)],
    3: [("h3", 1), ("h3", 2), ("h2", 0), ("h2", 1), ("h2", 2), ("h3", 0), ("y3", 1), ("y3", 0), ("y3", 2)],
    4: [("y4", 2), ("y4", 0), ("y4", 1)],
    5: [("h5", 0), ("h4", 0), ("h4", 1), ("h4", 2), ("h5", 1), ("h5", 2), ("y5", 0), ("y5", 2), ("y5", 1)],
    6: [("h6", 1), ("h7", 1), ("h7", 2), ("h6", 0), ("h7", 0), ("h6", 2), ("y6", 0), ("y6", 1), ("y6", 2)],
    7: [("h7", 2), ("h7", 1), ("h7", 0), ("y7", 2), ("y7", 1), ("y7", 0)],
    8: [("y8", 1), ("y8", 0), ("y8", 2)],
    9: [("h9", 1), ("h9", 0), ("h9", 2), ("h8", 0), ("h8", 1), ("y9", 1), ("h8", 2), ("y9", 2), ("y9", 0)],
    10: [("y10", 2), ("y10", 0), ("y10", 1)],
    11: [("h11", 2), ("h11", 1), ("h10", 1), ("h10", 2), ("h10", 0), ("h11", 0), ("y11", 2), ("y11", 1), ("y11", 0)],
}

SCRATCH = {"zero": ("sbuf", [128, TK], "float32"), "yy": ("sbuf", [128, TK], "bfloat16")}
for _i in range(NRANK):
    SCRATCH["xw%d" % _i] = ("sbuf", [128, TK + WK], "bfloat16")
    SCRATCH["h%d" % _i] = ("sbuf", [128, TK], "bfloat16")
for _i in range(NBANK):
    SCRATCH["p%d" % _i] = ("psum", [128, 512], "float32")
SEMAPHORES = ["zs", "sent", "st", "sy"] + ["mm%d" % _i for _i in range(NBANK)]
for _k in "xwh":
    SEMAPHORES += ["s%s%d" % (_k, _i) for _i in range(NRANK)]


def parts(it):
    return ["x" + it[2:], "w" + it[2:]] if it[:2] == "xw" else [it]


def bits(m):
    n = 0
    while m:
        n += m & 1
        m >>= 1
    return n


def rank_program(g, core, T, topo):
    rank = T.rank_of(core)
    if rank is None:
        return
    cores = list(T.cores)
    M = T.tables["MASK"]

    def sets(c):
        every, wide = ~0, 0
        for b in cores:
            if b != c and topo.may_write(c, b):
                every &= topo.mask(c, b)
                wide |= topo.mask(c, b)
        return {"A": every, "B": wide & ~every, "F": wide}

    def ap(it):
        j = it[2:] if it[:2] == "xw" else it[1:]
        if it[:2] == "xw":
            return T["xw" + j][:]
        if it[0] == "x":
            return T["xw" + j][:, 0:TK]
        if it[0] == "w":
            return T["xw" + j][:, TK:TK + WK]
        return T["h" + j][:]

    have = {"x%d" % rank: ("sx%d" % rank, 16), "w%d" % rank: ("sw%d" % rank, 16)}
    for s in CALLS:
        for it, ds in CALLS[s]:
            for d, gp in ds:
                if d == rank:
                    for p in parts(it):
                        have[p] = ("s" + parts(it)[0], bits(sets(cores[s])[gp]))
    outs = []
    for o, _ in MM[rank]:
        if o not in outs:
            outs.append(o)
            have[o] = ("sy", 1) if o[0] == "y" else ("s" + o, 1)

    def wait(q, it):
        for p in parts(it):
            q.wait_ge(T.sem[have[p][0]], have[p][1])

    g.sync.dma_start(ap("x%d" % rank), T.x[:]).then_inc(T.sem["sx%d" % rank], 16)
    g.sync.dma_start(ap("w%d" % rank), T.w[:]).then_inc(T.sem["sw%d" % rank], 16)
    g.vector.memset(T.zero[:], 0.0).then_inc(T.sem.zs, 1)
    g.vector.wait_ge(T.sem.zs, 1)

    mine = sets(core)
    total = 0
    for it, ds in CALLS[rank]:
        wait(g, it)
        groups = {}
        for d, gp in ds:
            b = cores[d]
            if not topo.may_write(core, b) or mine[gp] & ~topo.mask(core, b):
                raise ValueError("rank %d may not write to rank %d on engine set %s" % (rank, d, gp))
            groups.setdefault(mine[gp], []).append(b)
        trs = []
        for m in sorted(groups):
            ids = [topo.addr(b, core) for b in groups[m]]
            trs.append(RemoteDMATransfer(dst_ids=[DstId(rid=a[0], pnc=a[1]) for a in ids], dma_engine_mask=m,
                                         remote_sem=T.sem["s" + parts(it)[0]], srcs=[ap(it)],
                                         dsts=[ap(it) for _ in groups[m]]))
            total += bits(m)
        g.remote_dma_fused(trs, local_sem=T.sem.sent)
    g.wait_ge(T.sem.sent, total)

    seen = {}
    order = []
    for o, i in MM[rank]:
        j = int(o[1:])
        op = ("x" if o[0] == "h" else "h") + "%d" % M[j][i]
        ti = outs.index(o)
        n = seen.get(o, 0)
        seen[o] = n + 1
        if n == 0:
            wait(g.tensor, "w%d" % j)
        wait(g.tensor, op)
        g.tensor.matmul(T["p%d" % ti][:, 0:TK], T["xw%d" % j][:, TK + 128 * i:TK + 128 * i + 128], ap(op),
                        start=(n == 0), stop=(n == 2)).then_inc(T.sem["mm%d" % ti], 1)
        if n == 2:
            order.append(o)
    for o in order:
        ti = outs.index(o)
        g.vector.wait_ge(T.sem["mm%d" % ti], 3)
        dst = T.yy[:] if o[0] == "y" else ap(o)
        g.vector.tensor_tensor(dst, T["p%d" % ti][:, 0:TK], T.zero[:], AluOpType.max).then_inc(T.sem[have[o][0]], 1)
    g.sync.wait_ge(T.sem.sy, 1)
    g.sync.dma_start(T.y[:], T.yy[:]).then_inc(T.sem.st, 16)
    g.sync.wait_ge(T.sem.st, 16)
